import numpy as np
import ml_dtypes


def mxq(x, axis, fmt="e4m3"):
    dtype, down = {"e4m3": (ml_dtypes.float8_e4m3fn, 7), "e5m2": (ml_dtypes.float8_e5m2, 14)}[fmt]
    v = np.moveaxis(np.asarray(x, np.float32).astype(ml_dtypes.bfloat16).astype(np.float64), axis, -1)
    blocks = v.reshape(v.shape[:-1] + (-1, 32))
    amax = np.abs(blocks).max(-1, keepdims=True)
    byte = np.maximum(np.where(amax > 0, np.frexp(amax)[1] - 1 + 127, 0) - down, 1)
    scale = np.exp2(byte - 127.0)
    codes = (blocks / scale).astype(np.float32).astype(dtype).astype(np.float64)
    return np.moveaxis((codes * scale).reshape(v.shape), -1, axis)


WIDE = False


def mx_kscale(k):
    if not WIDE:
        return np.ones(k)
    levels = np.array([10, -10, 5, -5, 0])
    if k % 512:
        return np.exp2(np.random.permutation(np.resize(levels, k // 32))).repeat(32)
    a = np.empty((k // 512, 16))
    for p in range(k // 512):
        a[p, :8] = np.random.permutation(np.resize(levels, 8))
        for g in range(8):
            far = levels[np.abs(levels - a[p, g]) >= 10]
            a[p, g + 8] = far[np.random.randint(len(far))]
    return np.exp2(a.ravel()).repeat(32)


def f64(x):
    return np.asarray(x).astype(np.float64)


def striped(idx):
    return np.tile(np.asarray(idx).reshape(-1, 16).T, (8, 1)).astype(np.uint16)


def unstriped(offs):
    return offs[:16].T.reshape(-1).astype(np.int64)


E2M1 = np.array([0.0, 0.5, 1.0, 1.5, 2.0, 3.0, 4.0, 6.0, -0.0, -0.5, -1.0, -1.5, -2.0, -3.0, -4.0, -6.0])


def pack_weight(w, fmt):
    k, n = w.shape
    w = f64(np.asarray(w, np.float32).astype(ml_dtypes.bfloat16)).reshape(k // 32, 32, n)
    amax = np.abs(w).max(1)
    if fmt == "e4m3":
        byte = np.frexp(amax)[1] - 1 + 127 - 7
    else:
        mant, ex = np.frexp(amax / 6.0)
        byte = np.where(mant > 0.5, ex, ex - 1) + 127
    byte = np.clip(np.where(amax > 0, byte, 1), 1, 254)
    scaled = (w * np.exp2(127.0 - byte)[:, None, :]).reshape(k, n).astype(np.float32)
    by_word = np.ascontiguousarray(scaled.reshape(k // 512, 128, 4, n).transpose(0, 1, 3, 2))
    if fmt == "e4m3":
        words = by_word.astype(ml_dtypes.float8_e4m3fn).view(np.uint8)
    else:
        c = by_word.astype(ml_dtypes.float4_e2m1fn).view(np.uint8) & 0xF
        words = (c[..., 0::2] | (c[..., 1::2] << 4)).reshape(k // 512, 128, 2 * n)
    return np.ascontiguousarray(words), np.ascontiguousarray(byte.astype(np.uint8).reshape(k // 512, 16, n))


def unpack_weight(words, scales, fmt):
    g, _, n = scales.shape
    words = np.ascontiguousarray(words).reshape(g, 128, n, -1)
    if fmt == "e4m3":
        vals = words.view(ml_dtypes.float8_e4m3fn).astype(np.float64)
    else:
        nib = np.empty((g, 128, n, 4), np.uint8)
        nib[..., 0::2] = words & 0xF
        nib[..., 1::2] = words >> 4
        vals = E2M1[nib]
    vals = vals * np.repeat(np.exp2(scales.astype(np.float64) - 127.0), 8, axis=1)[..., None]
    return vals.transpose(0, 1, 3, 2).reshape(g * 512, n)


B, N, T, D, NQ = 1, 512, 2048, 1024, 512
SEG = 16


def setup_inputs():
    n = np.random.standard_normal
    pages = np.random.permutation(T // 64)[:B * N // 64]
    idx = (pages[:, None] * 64 + np.arange(64)[None, :]).reshape(-1)
    s = mx_kscale(D)[:, None]
    kp = pack_weight(n((D, T)) / s, "e2m1")
    return {
        "qT": (n((B, D, NQ)) * s * (1.00 / np.sqrt(D))).astype(np.float32),
        "k_words": np.ascontiguousarray(kp[0].reshape(1, 2, 128, T, 2).transpose(0, 2, 3, 1, 4)).reshape(1, 128, T, 4),
        "k_scales": kp[1],
        "ls": (np.random.uniform(7.8, 8.4, (B, 1, NQ))).astype(np.float32),
        "offs": striped(idx),
    }


def reference(qT, k_words, k_scales, ls, offs):
    idx = unstriped(offs)
    pick = lambda x, which: x[:, which].reshape(x.shape[0], B, -1).transpose(1, 0, 2)
    k = unpack_weight(k_words.reshape(1, 128, T, 2, 2).transpose(0, 3, 1, 2, 4).reshape(2, 128, 2 * T), k_scales, "e2m1")
    kg = pick(k, idx)
    qq = mxq(f64(qT), 1, "e4m3")
    a = kg.transpose(0, 2, 1) @ qq
    y = np.exp(a - f64(ls)).reshape(B, N, NQ // SEG, SEG).sum(-1)
    return y

@@ -1,0 +1,161 @@
+from contextlib import ExitStack
+
+import concourse.mybir as mybir
+from concourse.masks import make_identity
+
+F32 = mybir.dt.float32
+BF16 = mybir.dt.bfloat16
+I32 = mybir.dt.int32
+U32 = mybir.dt.uint32
+U16 = mybir.dt.uint16
+U8 = mybir.dt.uint8
+FP8X4 = mybir.dt.float8_e4m3fn_x4
+FP4X4 = mybir.dt.float4_e2m1fn_x4
+EXP = mybir.ActivationFunctionType.Exp
+
+P = 128
+PACK = 4
+K_PASS = P * PACK
+SLOTS, TOKENS, D, NQ, SEG = 512, 2048, 1024, 512, 16
+PASSES = D // K_PASS
+HALVES = 2
+HALF = NQ // HALVES
+TILES = HALF // P
+RUN = 4
+KEY_TILES = SLOTS // P
+FLOPS = 2 * SLOTS * D * NQ
+
+
+def tile_attend_snapkv_kernel(tc, qT, k_words, k_scales, ls, offs, out):
+    nc = tc.nc
+    with ExitStack() as ctx:
+        keep = ctx.enter_context(tc.tile_pool(name="keep", bufs=1))
+        psum = ctx.enter_context(tc.psum_pool(name="psum", bufs=1))
+
+        offsets = keep.tile([P, SLOTS // 16], U16, name="offsets")
+        words = keep.tile([P, TOKENS], I32, name="words", align_bytes=64)
+        scales = keep.tile([P, PASSES * TOKENS // 4], I32, name="scales", align_bytes=64)
+        ls_rows = keep.tile([P, HALF], F32, name="ls_rows")
+        ident = keep.tile([P, P], F32, name="ident")
+        warm = keep.tile([P, 8], F32, name="warm")
+        warm_out = keep.tile([P, 8], F32, name="warm_out")
+
+        nc.vector.memset(scales[:], 0)
+        nc.vector.memset(ls_rows[:], 0.0)
+        nc.vector.memset(warm[:], 0.0)
+        nc.scalar.activation(warm_out[:], warm[:], EXP)
+
+        nc.sync.dma_start(out=words[:], in_=k_words[0].rearrange("p t b -> p (t b)").bitcast(I32))
+        nc.sync.dma_start(offsets[:], offs)
+        make_identity(nc, ident[:])
+        scale_rows = k_scales.bitcast(I32).rearrange("o (q r) c -> r q o c", r=4)
+        for r in range(4):
+            nc.scalar.dma_start(
+                out=scales[r:P:32, :].rearrange("q (o c) -> q o c", o=PASSES), in_=scale_rows[r]
+            )
+        nc.sync.dma_start(out=ls_rows[0:HALVES, :], in_=ls[0, 0].rearrange("(h c) -> h c", h=HALVES))
+
+        raw = {}
+        for half in range(HALVES):
+            for o in range(PASSES):
+                raw[half, o] = keep.tile([P, PACK, HALF], F32, name="raw%d%d" % (half, o))
+                nc.sync.dma_start(
+                    out=raw[half, o][:],
+                    in_=qT[0, o * K_PASS : (o + 1) * K_PASS, half * HALF : (half + 1) * HALF].rearrange(
+                        "(p j) w -> p j w", j=PACK
+                    ),
+                )
+
+        neg_rows = keep.tile([P, TILES, P], F32, name="neg_rows")
+        nc.vector.tensor_scalar_mul(
+            neg_rows[:].rearrange("p t (g i) -> p t g i", i=RUN),
+            ls_rows[:].rearrange("p (g t i) -> p t g i", t=TILES, i=RUN),
+            -1.0,
+        )
+        ls_bank = psum.tile([P, TILES, P], F32, name="ls_bank")
+        for t in range(TILES):
+            nc.tensor.transpose(ls_bank[:, t, :], neg_rows[:, t, :], ident[:])
+        bias = keep.tile([P, TILES, HALVES], F32, name="bias")
+        nc.vector.tensor_copy(bias[:], ls_bank[:, :, 0:HALVES])
+
+        picked = keep.tile([P, SLOTS], U32, name="picked", align_bytes=64)
+        nc.vector.tensor_copy(picked[:], words[:].bitcast(U32).indirect(offsets[:]))
+        picked_halves = picked[:].bitcast(U16).rearrange("p (n o) -> p o n", o=PASSES)
+        scale_bytes = scales[:].bitcast(U8)
+        key_words, key_scales = [], []
+        for o in range(PASSES):
+            kw = keep.tile([P, 2 * SLOTS], U8, name="key_words%d" % o, align_bytes=64)
+            nc.vector.tensor_copy(kw[:].bitcast(U16), picked_halves[:, o, :])
+            key_words.append(kw)
+            ks = keep.tile([P, SLOTS], U8, name="key_scales%d" % o, align_bytes=64)
+            nc.vector.tensor_copy(ks[:], scale_bytes[:, o * TOKENS : (o + 1) * TOKENS].indirect(offsets[:]))
+            key_scales.append(ks)
+
+        on_scalar = [(0, 0, 0), (0, 0, 1), (0, 1, 0), (1, 1, 1)]
+        scores = {}
+        for half in range(HALVES):
+            for t in range(TILES):
+                scores[half, t] = psum.tile([P, SLOTS], F32, name="scores%d%d" % (half, t))
+
+        def multiply(half, o, t):
+            tag = "%d%d%d" % (half, o, t)
+            grouped = keep.tile([P, P, PACK], BF16, name="grouped" + tag, align_bytes=64)
+            src = raw[half, o][:].rearrange("p j (g t i) -> p t g j i", t=TILES, i=RUN)[:, t]
+            dst = grouped[:].rearrange("p (g i) j -> p g j i", i=RUN)
+            if (half, o, t) in on_scalar:
+                nc.scalar.copy(dst, src)
+            else:
+                nc.vector.tensor_copy(dst, src)
+            codes = keep.tile([P, P], U32, name="codes" + tag, align_bytes=64)
+            plane = keep.tile([P, P], U8, name="plane" + tag, align_bytes=64)
+            nc.vector.quantize_mx(
+                out=codes[:].bitcast(FP8X4), scales=plane[:], in_=grouped[:].rearrange("p c j -> p (c j)")
+            )
+            nc.tensor.matmul_mx(
+                out=scores[half, t][:],
+                lhsT=codes[:].bitcast(FP8X4),
+                lhsT_scale=plane[:],
+                rhs=key_words[o][:].bitcast(FP4X4),
+                rhs_scale=key_scales[o][:],
+                start=(o == 0),
+                stop=(o == PASSES - 1),
+            )
+
+        def weigh(half):
+            turned = psum.tile([P, KEY_TILES, P], F32, name="turned%d" % half)
+            for t in range(TILES):
+                weights = keep.tile([P, SLOTS], F32, name="weights%d%d" % (half, t))
+                nc.scalar.activation(weights[:], scores[half, t][:], EXP, bias=bias[:, t, half : half + 1])
+                for kt in range(KEY_TILES):
+                    nc.tensor.matmul(
+                        turned[:, kt, :],
+                        lhsT=weights[:, kt * P : (kt + 1) * P],
+                        rhs=ident[:],
+                        start=(t == 0 and kt == 0),
+                        stop=(t == TILES - 1 and kt == KEY_TILES - 1),
+                        is_transpose=True,
+                    )
+            return turned
+
+        def store(half, turned):
+            segs = HALF // SEG
+            result = keep.tile([P, KEY_TILES, segs], F32, name="result%d" % half)
+            nc.vector.tensor_reduce(
+                result[:].rearrange("p k s -> p (k s)"),
+                turned[:].rearrange("p k (s e) -> p (k s) e", s=segs),
+                axis=mybir.AxisListType.X,
+                op=mybir.AluOpType.add,
+            )
+            nc.sync.dma_start(
+                out=out[0, :, half * segs : (half + 1) * segs].rearrange("(k p) s -> p k s", p=P), in_=result[:]
+            )
+
+        for o in range(PASSES):
+            for t in range(TILES):
+                multiply(0, o, t)
+        turned0 = weigh(0)
+        for o in range(PASSES):
+            for t in range(TILES):
+                multiply(1, o, t)
+        store(0, turned0)
+        store(1, weigh(1))

@@ -12,17 +12,16 @@ U8 = mybir.dt.uint8
 FP8X4 = mybir.dt.float8_e4m3fn_x4
 FP4X4 = mybir.dt.float4_e2m1fn_x4
 EXP = mybir.ActivationFunctionType.Exp
+COPY = mybir.ActivationFunctionType.Copy
 
 P = 128
 PACK = 4
 K_PASS = P * PACK
 SLOTS, TOKENS, D, NQ, SEG = 512, 2048, 1024, 512, 16
 PASSES = D // K_PASS
-HALVES = 2
-HALF = NQ // HALVES
-TILES = HALF // P
-RUN = 4
+HALF = NQ // 2
 KEY_TILES = SLOTS // P
+SEGS = NQ // SEG
 FLOPS = 2 * SLOTS * D * NQ
 
 
@@ -40,69 +39,76 @@ def tile_attend_snapkv_kernel(tc, qT, k_words, k_scales, ls, offs, out):
         warm = keep.tile([P, 8], F32, name="warm")
         warm_out = keep.tile([P, 8], F32, name="warm_out")
 
-        nc.vector.memset(scales[:], 0)
-        nc.vector.memset(ls_rows[:], 0.0)
+        nc.gpsimd.memset(scales[:, 0:512], 0)
+        nc.vector.memset(scales[:, 512:], 0)
         nc.vector.memset(warm[:], 0.0)
         nc.scalar.activation(warm_out[:], warm[:], EXP)
-
-        nc.sync.dma_start(out=words[:], in_=k_words[0].rearrange("p t b -> p (t b)").bitcast(I32))
-        nc.sync.dma_start(offsets[:], offs)
+        nc.vector.memset(ls_rows[:], 0.0)
         make_identity(nc, ident[:])
+
+        word_rows = k_words[0].rearrange("p t b -> p (t b)").bitcast(I32)
+        nc.sync.dma_start(out=words[:, 0:768], in_=word_rows[:, 0:768])
+        nc.sync.dma_start(offsets[:], offs)
         scale_rows = k_scales.bitcast(I32).rearrange("o (q r) c -> r q o c", r=4)
         for r in range(4):
-            nc.scalar.dma_start(
+            nc.sync.dma_start(
                 out=scales[r:P:32, :].rearrange("q (o c) -> q o c", o=PASSES), in_=scale_rows[r]
             )
-        nc.sync.dma_start(out=ls_rows[0:HALVES, :], in_=ls[0, 0].rearrange("(h c) -> h c", h=HALVES))
+        nc.sync.dma_start(out=words[:, 768:], in_=word_rows[:, 768:])
+        nc.scalar.dma_start(out=ls_rows[0:2, :], in_=ls[0, 0].rearrange("(h c) -> h c", h=2))
 
-        raw = {}
-        for half in range(HALVES):
+        def load(name, o, first, count):
+            raw = keep.tile([P, PACK, count], F32, name=name)
+            nc.sync.dma_start(
+                out=raw[:],
+                in_=qT[0, o * K_PASS : (o + 1) * K_PASS, first : first + count].rearrange("(p j) w -> p j w", j=PACK),
+            )
+            return raw
+
+        low = [load("low%d" % o, o, 0, HALF) for o in range(PASSES)]
+        high0 = load("high0", 0, HALF, HALF)
+        high1 = [load("high1%d" % t, 1, HALF + t * P, P) for t in range(2)]
+
+        source = {}
+        for t in range(2):
             for o in range(PASSES):
-                raw[half, o] = keep.tile([P, PACK, HALF], F32, name="raw%d%d" % (half, o))
-                nc.sync.dma_start(
-                    out=raw[half, o][:],
-                    in_=qT[0, o * K_PASS : (o + 1) * K_PASS, half * HALF : (half + 1) * HALF].rearrange(
-                        "(p j) w -> p j w", j=PACK
-                    ),
-                )
+                source[t, o] = low[o][:].rearrange("p j (g i t) -> p t g j i", t=2, i=2)[:, t]
+            source[2 + t, 0] = high0[:, :, t * P : (t + 1) * P].rearrange("p j (g i) -> p g j i", i=4)
+            source[2 + t, 1] = high1[t][:].rearrange("p j (g i) -> p g j i", i=4)
 
-        neg_rows = keep.tile([P, TILES, P], F32, name="neg_rows")
-        nc.vector.tensor_scalar_mul(
-            neg_rows[:].rearrange("p t (g i) -> p t g i", i=RUN),
-            ls_rows[:].rearrange("p (g t i) -> p t g i", t=TILES, i=RUN),
-            -1.0,
-        )
-        ls_bank = psum.tile([P, TILES, P], F32, name="ls_bank")
-        for t in range(TILES):
-            nc.tensor.transpose(ls_bank[:, t, :], neg_rows[:, t, :], ident[:])
-        bias = keep.tile([P, TILES, HALVES], F32, name="bias")
-        nc.vector.tensor_copy(bias[:], ls_bank[:, :, 0:HALVES])
+        ls_bank = psum.tile([P, 4, P], F32, name="ls_bank", tag="last")
+        for t in range(2):
+            nc.tensor.transpose(ls_bank[:, t, :], ls_rows[:, t:HALF:2], ident[:])
+            nc.tensor.transpose(ls_bank[:, 2 + t, :], ls_rows[:, t * P : (t + 1) * P], ident[:])
+        idle_bank = psum.tile([P, 4, P], F32, name="idle_bank", tag="turned_2")
+        for u in range(28):
+            nc.tensor.transpose(idle_bank[:, u % 4, :], ls_rows[:, 0:P], ident[:])
+        bias = keep.tile([P, 4, 2], F32, name="bias")
+        nc.scalar.activation(bias[:], ls_bank[:, :, 0:2], COPY, scale=-1.0)
 
+        scale_bytes = scales[:].bitcast(U8)
+        key_words, key_scales = [], []
+        for o in range(PASSES):
+            ks = keep.tile([P, SLOTS], U8, name="key_scales%d" % o, align_bytes=64)
+            nc.vector.tensor_copy(ks[:], scale_bytes[:, o * TOKENS : (o + 1) * TOKENS].indirect(offsets[:]))
+            key_scales.append(ks)
         picked = keep.tile([P, SLOTS], U32, name="picked", align_bytes=64)
         nc.vector.tensor_copy(picked[:], words[:].bitcast(U32).indirect(offsets[:]))
         picked_halves = picked[:].bitcast(U16).rearrange("p (n o) -> p o n", o=PASSES)
-        scale_bytes = scales[:].bitcast(U8)
-        key_words, key_scales = [], []
         for o in range(PASSES):
             kw = keep.tile([P, 2 * SLOTS], U8, name="key_words%d" % o, align_bytes=64)
             nc.vector.tensor_copy(kw[:].bitcast(U16), picked_halves[:, o, :])
             key_words.append(kw)
-            ks = keep.tile([P, SLOTS], U8, name="key_scales%d" % o, align_bytes=64)
-            nc.vector.tensor_copy(ks[:], scale_bytes[:, o * TOKENS : (o + 1) * TOKENS].indirect(offsets[:]))
-            key_scales.append(ks)
 
-        on_scalar = [(0, 0, 0), (0, 0, 1), (0, 1, 0), (1, 1, 1)]
-        scores = {}
-        for half in range(HALVES):
-            for t in range(TILES):
-                scores[half, t] = psum.tile([P, SLOTS], F32, name="scores%d%d" % (half, t))
+        on_scalar = [(0, 0), (1, 0), (0, 1), (3, 0)]
+        scores = [psum.tile([P, SLOTS], F32, name="scores%d" % t) for t in range(4)]
 
-        def multiply(half, o, t):
-            tag = "%d%d%d" % (half, o, t)
-            grouped = keep.tile([P, P, PACK], BF16, name="grouped" + tag, align_bytes=64)
-            src = raw[half, o][:].rearrange("p j (g t i) -> p t g j i", t=TILES, i=RUN)[:, t]
-            dst = grouped[:].rearrange("p (g i) j -> p g j i", i=RUN)
-            if (half, o, t) in on_scalar:
+        def multiply(t, o):
+            tag = "%d%d" % (t, o)
+            grouped = keep.tile([P, P, PACK], BF16, name="grouped" + tag, tag="grouped" + tag, align_bytes=64)
+            src = source[t, o]
+            dst = grouped[:].rearrange("p (g i) j -> p g j i", i=src.shape[3])
+            if (t, o) in on_scalar:
                 nc.scalar.copy(dst, src)
             else:
                 nc.vector.tensor_copy(dst, src)
@@ -112,7 +118,7 @@ def tile_attend_snapkv_kernel(tc, qT, k_words, k_scales, ls, offs, out):
                 out=codes[:].bitcast(FP8X4), scales=plane[:], in_=grouped[:].rearrange("p c j -> p (c j)")
             )
             nc.tensor.matmul_mx(
-                out=scores[half, t][:],
+                out=scores[t][:],
                 lhsT=codes[:].bitcast(FP8X4),
                 lhsT_scale=plane[:],
                 rhs=key_words[o][:].bitcast(FP4X4),
@@ -121,41 +127,54 @@ def tile_attend_snapkv_kernel(tc, qT, k_words, k_scales, ls, offs, out):
                 stop=(o == PASSES - 1),
             )
 
-        def weigh(half):
-            turned = psum.tile([P, KEY_TILES, P], F32, name="turned%d" % half)
-            for t in range(TILES):
-                weights = keep.tile([P, SLOTS], F32, name="weights%d%d" % (half, t))
-                nc.scalar.activation(weights[:], scores[half, t][:], EXP, bias=bias[:, t, half : half + 1])
-                for kt in range(KEY_TILES):
+        def weigh(tiles, kts, turned):
+            for t in tiles:
+                weights = keep.tile([P, len(kts), P], F32, name="weights%d%d" % (t, kts[0]))
+                nc.scalar.activation(
+                    weights[:],
+                    scores[t][:].rearrange("p (n k) -> p k n", k=KEY_TILES)[:, kts[0] : kts[-1] + 1, :],
+                    EXP,
+                    bias=bias[:, t, t // 2 : t // 2 + 1],
+                )
+                for u in range(len(kts)):
                     nc.tensor.matmul(
-                        turned[:, kt, :],
-                        lhsT=weights[:, kt * P : (kt + 1) * P],
+                        turned[:, u, :],
+                        lhsT=weights[:, u, :],
                         rhs=ident[:],
-                        start=(t == 0 and kt == 0),
-                        stop=(t == TILES - 1 and kt == KEY_TILES - 1),
+                        start=(t == tiles[0] and u == 0),
+                        stop=(t == tiles[-1] and u == len(kts) - 1),
                         is_transpose=True,
                     )
-            return turned
 
-        def store(half, turned):
-            segs = HALF // SEG
-            result = keep.tile([P, KEY_TILES, segs], F32, name="result%d" % half)
+        def add_up(result, tiles, kts, turned):
+            segs = len(tiles) * P // SEG
+            first = tiles[0] * P // SEG
             nc.vector.tensor_reduce(
-                result[:].rearrange("p k s -> p (k s)"),
-                turned[:].rearrange("p k (s e) -> p (k s) e", s=segs),
+                result[:, kts[0] : kts[-1] + 1, first : first + segs],
+                turned[:, 0 : len(kts), :].rearrange("p k (s e) -> p k s e", s=segs),
                 axis=mybir.AxisListType.X,
                 op=mybir.AluOpType.add,
             )
-            nc.sync.dma_start(
-                out=out[0, :, half * segs : (half + 1) * segs].rearrange("(k p) s -> p k s", p=P), in_=result[:]
-            )
 
+        every = list(range(KEY_TILES))
         for o in range(PASSES):
-            for t in range(TILES):
-                multiply(0, o, t)
-        turned0 = weigh(0)
-        for o in range(PASSES):
-            for t in range(TILES):
-                multiply(1, o, t)
-        store(0, turned0)
-        store(1, weigh(1))
+            for t in range(2):
+                multiply(t, o)
+        turned_low = psum.tile([P, KEY_TILES, P], F32, name="turned_low")
+        weigh([0, 1], every, turned_low)
+        multiply(2, 0)
+        multiply(3, 0)
+        multiply(2, 1)
+        multiply(3, 1)
+        result = keep.tile([P, KEY_TILES, SEGS], F32, name="result", tag="grouped31", align_bytes=64)
+        add_up(result, [0, 1], every, turned_low)
+        turned_2 = psum.tile([P, KEY_TILES, P], F32, name="turned_2", tag="turned_2")
+        weigh([2], every, turned_2)
+        add_up(result, [2], every, turned_2)
+        turned_3a = psum.tile([P, KEY_TILES, P], F32, name="turned_3a")
+        weigh([3], every[:2], turned_3a)
+        turned_3b = psum.tile([P, KEY_TILES, P], F32, name="turned_3b", tag="last")
+        weigh([3], every[2:], turned_3b)
+        add_up(result, [3], every[:2], turned_3a)
+        add_up(result, [3], every[2:], turned_3b)
+        nc.sync.dma_start(out=out[0].rearrange("(n k) s -> n k s", k=KEY_TILES), in_=result[:])

from contextlib import ExitStack

import concourse.mybir as mybir
from concourse.masks import make_identity

F32 = mybir.dt.float32
BF16 = mybir.dt.bfloat16
I32 = mybir.dt.int32
U32 = mybir.dt.uint32
U16 = mybir.dt.uint16
U8 = mybir.dt.uint8
FP8X4 = mybir.dt.float8_e4m3fn_x4
FP4X4 = mybir.dt.float4_e2m1fn_x4
EXP = mybir.ActivationFunctionType.Exp
COPY = mybir.ActivationFunctionType.Copy

P = 128
PACK = 4
K_PASS = P * PACK
SLOTS, TOKENS, D, NQ, SEG = 512, 2048, 1024, 512, 16
PASSES = D // K_PASS
HALF = NQ // 2
KEY_TILES = SLOTS // P
SEGS = NQ // SEG
FLOPS = 2 * SLOTS * D * NQ


def tile_attend_snapkv_kernel(tc, qT, k_words, k_scales, ls, offs, out):
    nc = tc.nc
    with ExitStack() as ctx:
        keep = ctx.enter_context(tc.tile_pool(name="keep", bufs=1))
        psum = ctx.enter_context(tc.psum_pool(name="psum", bufs=1))

        offsets = keep.tile([P, SLOTS // 16], U16, name="offsets")
        words = keep.tile([P, TOKENS], I32, name="words", align_bytes=64)
        scales = keep.tile([P, PASSES * TOKENS // 4], I32, name="scales", align_bytes=64)
        ls_rows = keep.tile([P, HALF], F32, name="ls_rows")
        ident = keep.tile([P, P], F32, name="ident")
        warm = keep.tile([P, 8], F32, name="warm")
        warm_out = keep.tile([P, 8], F32, name="warm_out")

        nc.gpsimd.memset(scales[:, 0:512], 0)
        nc.vector.memset(scales[:, 512:], 0)
        nc.vector.memset(warm[:], 0.0)
        nc.scalar.activation(warm_out[:], warm[:], EXP)
        nc.vector.memset(ls_rows[:], 0.0)
        make_identity(nc, ident[:])

        word_rows = k_words[0].rearrange("p t b -> p (t b)").bitcast(I32)
        nc.sync.dma_start(out=words[:, 0:768], in_=word_rows[:, 0:768])
        nc.sync.dma_start(offsets[:], offs)
        scale_rows = k_scales.bitcast(I32).rearrange("o (q r) c -> r q o c", r=4)
        for r in range(4):
            nc.sync.dma_start(
                out=scales[r:P:32, :].rearrange("q (o c) -> q o c", o=PASSES), in_=scale_rows[r]
            )
        nc.sync.dma_start(out=words[:, 768:], in_=word_rows[:, 768:])
        nc.scalar.dma_start(out=ls_rows[0:2, :], in_=ls[0, 0].rearrange("(h c) -> h c", h=2))

        def load(name, o, first, count):
            raw = keep.tile([P, PACK, count], F32, name=name)
            nc.sync.dma_start(
                out=raw[:],
                in_=qT[0, o * K_PASS : (o + 1) * K_PASS, first : first + count].rearrange("(p j) w -> p j w", j=PACK),
            )
            return raw

        low = [load("low%d" % o, o, 0, HALF) for o in range(PASSES)]
        high0 = load("high0", 0, HALF, HALF)
        high1 = [load("high1%d" % t, 1, HALF + t * P, P) for t in range(2)]

        source = {}
        for t in range(2):
            for o in range(PASSES):
                source[t, o] = low[o][:].rearrange("p j (g i t) -> p t g j i", t=2, i=2)[:, t]
            source[2 + t, 0] = high0[:, :, t * P : (t + 1) * P].rearrange("p j (g i) -> p g j i", i=4)
            source[2 + t, 1] = high1[t][:].rearrange("p j (g i) -> p g j i", i=4)

        ls_bank = psum.tile([P, 4, P], F32, name="ls_bank", tag="last")
        for t in range(2):
            nc.tensor.transpose(ls_bank[:, t, :], ls_rows[:, t:HALF:2], ident[:])
            nc.tensor.transpose(ls_bank[:, 2 + t, :], ls_rows[:, t * P : (t + 1) * P], ident[:])
        idle_bank = psum.tile([P, 4, P], F32, name="idle_bank", tag="turned_2")
        for u in range(28):
            nc.tensor.transpose(idle_bank[:, u % 4, :], ls_rows[:, 0:P], ident[:])
        bias = keep.tile([P, 4, 2], F32, name="bias")
        nc.scalar.activation(bias[:], ls_bank[:, :, 0:2], COPY, scale=-1.0)

        scale_bytes = scales[:].bitcast(U8)
        key_words, key_scales = [], []
        for o in range(PASSES):
            ks = keep.tile([P, SLOTS], U8, name="key_scales%d" % o, align_bytes=64)
            nc.vector.tensor_copy(ks[:], scale_bytes[:, o * TOKENS : (o + 1) * TOKENS].indirect(offsets[:]))
            key_scales.append(ks)
        picked = keep.tile([P, SLOTS], U32, name="picked", align_bytes=64)
        nc.vector.tensor_copy(picked[:], words[:].bitcast(U32).indirect(offsets[:]))
        picked_halves = picked[:].bitcast(U16).rearrange("p (n o) -> p o n", o=PASSES)
        for o in range(PASSES):
            kw = keep.tile([P, 2 * SLOTS], U8, name="key_words%d" % o, align_bytes=64)
            nc.vector.tensor_copy(kw[:].bitcast(U16), picked_halves[:, o, :])
            key_words.append(kw)

        on_scalar = [(0, 0), (1, 0), (0, 1), (3, 0)]
        scores = [psum.tile([P, SLOTS], F32, name="scores%d" % t) for t in range(4)]

        def multiply(t, o):
            tag = "%d%d" % (t, o)
            grouped = keep.tile([P, P, PACK], BF16, name="grouped" + tag, tag="grouped" + tag, align_bytes=64)
            src = source[t, o]
            dst = grouped[:].rearrange("p (g i) j -> p g j i", i=src.shape[3])
            if (t, o) in on_scalar:
                nc.scalar.copy(dst, src)
            else:
                nc.vector.tensor_copy(dst, src)
            codes = keep.tile([P, P], U32, name="codes" + tag, align_bytes=64)
            plane = keep.tile([P, P], U8, name="plane" + tag, align_bytes=64)
            nc.vector.quantize_mx(
                out=codes[:].bitcast(FP8X4), scales=plane[:], in_=grouped[:].rearrange("p c j -> p (c j)")
            )
            nc.tensor.matmul_mx(
                out=scores[t][:],
                lhsT=codes[:].bitcast(FP8X4),
                lhsT_scale=plane[:],
                rhs=key_words[o][:].bitcast(FP4X4),
                rhs_scale=key_scales[o][:],
                start=(o == 0),
                stop=(o == PASSES - 1),
            )

        def weigh(tiles, kts, turned):
            for t in tiles:
                weights = keep.tile([P, len(kts), P], F32, name="weights%d%d" % (t, kts[0]))
                nc.scalar.activation(
                    weights[:],
                    scores[t][:].rearrange("p (n k) -> p k n", k=KEY_TILES)[:, kts[0] : kts[-1] + 1, :],
                    EXP,
                    bias=bias[:, t, t // 2 : t // 2 + 1],
                )
                for u in range(len(kts)):
                    nc.tensor.matmul(
                        turned[:, u, :],
                        lhsT=weights[:, u, :],
                        rhs=ident[:],
                        start=(t == tiles[0] and u == 0),
                        stop=(t == tiles[-1] and u == len(kts) - 1),
                        is_transpose=True,
                    )

        def add_up(result, tiles, kts, turned):
            segs = len(tiles) * P // SEG
            first = tiles[0] * P // SEG
            nc.vector.tensor_reduce(
                result[:, kts[0] : kts[-1] + 1, first : first + segs],
                turned[:, 0 : len(kts), :].rearrange("p k (s e) -> p k s e", s=segs),
                axis=mybir.AxisListType.X,
                op=mybir.AluOpType.add,
            )

        every = list(range(KEY_TILES))
        for o in range(PASSES):
            for t in range(2):
                multiply(t, o)
        turned_low = psum.tile([P, KEY_TILES, P], F32, name="turned_low")
        weigh([0, 1], every, turned_low)
        multiply(2, 0)
        multiply(3, 0)
        multiply(2, 1)
        multiply(3, 1)
        result = keep.tile([P, KEY_TILES, SEGS], F32, name="result", tag="grouped31", align_bytes=64)
        add_up(result, [0, 1], every, turned_low)
        turned_2 = psum.tile([P, KEY_TILES, P], F32, name="turned_2", tag="turned_2")
        weigh([2], every, turned_2)
        add_up(result, [2], every, turned_2)
        turned_3a = psum.tile([P, KEY_TILES, P], F32, name="turned_3a")
        weigh([3], every[:2], turned_3a)
        turned_3b = psum.tile([P, KEY_TILES, P], F32, name="turned_3b", tag="last")
        weigh([3], every[2:], turned_3b)
        add_up(result, [3], every[:2], turned_3a)
        add_up(result, [3], every[2:], turned_3b)
        nc.sync.dma_start(out=out[0].rearrange("(n k) s -> n k s", k=KEY_TILES), in_=result[:])
